import numpy as np
import ml_dtypes


def mxq(x, axis, fmt="e4m3"):
    dtype, down = {"e4m3": (ml_dtypes.float8_e4m3fn, 7), "e5m2": (ml_dtypes.float8_e5m2, 14)}[fmt]
    v = np.moveaxis(np.asarray(x, np.float32).astype(ml_dtypes.bfloat16).astype(np.float64), axis, -1)
    blocks = v.reshape(v.shape[:-1] + (-1, 32))
    amax = np.abs(blocks).max(-1, keepdims=True)
    byte = np.maximum(np.where(amax > 0, np.frexp(amax)[1] - 1 + 127, 0) - down, 1)
    scale = np.exp2(byte - 127.0)
    codes = (blocks / scale).astype(np.float32).astype(dtype).astype(np.float64)
    return np.moveaxis((codes * scale).reshape(v.shape), -1, axis)


WIDE = False


def mx_kscale(k):
    if not WIDE:
        return np.ones(k)
    levels = np.array([10, -10, 5, -5, 0])
    if k % 512:
        return np.exp2(np.random.permutation(np.resize(levels, k // 32))).repeat(32)
    a = np.empty((k // 512, 16))
    for p in range(k // 512):
        a[p, :8] = np.random.permutation(np.resize(levels, 8))
        for g in range(8):
            far = levels[np.abs(levels - a[p, g]) >= 10]
            a[p, g + 8] = far[np.random.randint(len(far))]
    return np.exp2(a.ravel()).repeat(32)


def f64(x):
    return np.asarray(x).astype(np.float64)


def striped(idx):
    return np.tile(idx.reshape(-1, 16).T, (8, 1)).astype(np.uint16)


def unstriped(offs):
    return offs[:16].T.reshape(-1).astype(np.int64)


E2M1 = np.array([0.0, 0.5, 1.0, 1.5, 2.0, 3.0, 4.0, 6.0, -0.0, -0.5, -1.0, -1.5, -2.0, -3.0, -4.0, -6.0])


def pack_weight(w, fmt):
    k, n = w.shape
    w = f64(np.asarray(w, np.float32).astype(ml_dtypes.bfloat16)).reshape(k // 32, 32, n)
    amax = np.abs(w).max(1)
    if fmt == "e4m3":
        byte = np.frexp(amax)[1] - 1 + 127 - 7
    else:
        mant, ex = np.frexp(amax / 6.0)
        byte = np.where(mant > 0.5, ex, ex - 1) + 127
    byte = np.clip(np.where(amax > 0, byte, 1), 1, 254)
    scaled = (w * np.exp2(127.0 - byte)[:, None, :]).reshape(k, n).astype(np.float32)
    by_word = np.ascontiguousarray(scaled.reshape(k // 512, 128, 4, n).transpose(0, 1, 3, 2))
    if fmt == "e4m3":
        words = by_word.astype(ml_dtypes.float8_e4m3fn).view(np.uint8)
    else:
        c = by_word.astype(ml_dtypes.float4_e2m1fn).view(np.uint8) & 0xF
        words = (c[..., 0::2] | (c[..., 1::2] << 4)).reshape(k // 512, 128, 2 * n)
    return np.ascontiguousarray(words), np.ascontiguousarray(byte.astype(np.uint8).reshape(k // 512, 16, n))


def unpack_weight(words, scales, fmt):
    g, _, n = scales.shape
    words = np.ascontiguousarray(words).reshape(g, 128, n, -1)
    if fmt == "e4m3":
        vals = words.view(ml_dtypes.float8_e4m3fn).astype(np.float64)
    else:
        nib = np.empty((g, 128, n, 4), np.uint8)
        nib[..., 0::2] = words & 0xF
        nib[..., 1::2] = words >> 4
        vals = E2M1[nib]
    vals = vals * np.repeat(np.exp2(scales.astype(np.float64) - 127.0), 8, axis=1)[..., None]
    return vals.transpose(0, 1, 3, 2).reshape(g * 512, n)


def relu(v):
    return np.maximum(v, 0.0)


K, T, E, C, N = 512, 640, 5, 256, 512
M = 512


def by_expert(wq, xq):
    return np.concatenate([wq[e].T @ xq[:, e * C:(e + 1) * C] for e in range(E)], axis=1)


def setup_inputs():
    n = np.random.standard_normal
    s = mx_kscale(K)[:, None]
    v = mx_kscale(N)
    first = np.random.permutation(np.repeat(np.arange(E), T // E))
    second = (first + 1 + np.random.permutation(np.repeat(np.arange(E - 1), -(-T // (E - 1)))[:T])) % E
    while np.bincount(second, minlength=E).max() != T // E:
        load = np.bincount(second, minlength=E); hi, lo = int(load.argmax()), int(load.argmin())
        t = np.flatnonzero((second == hi) & (first != lo))[0]; second[t] = lo
    slot_token = np.empty(E * C, np.int64); pos = np.empty((2, T), np.int64); fill = np.zeros(E, np.int64)
    place = np.stack([np.random.permutation(C) for _ in range(E)])
    for r, deal in enumerate((first, second)):
        for t in np.random.permutation(T):
            e = deal[t]; j = e * C + place[e, fill[e]]; fill[e] += 1; slot_token[j] = t; pos[r, t] = j
    g = np.random.uniform(0.2, 0.8, T)
    x = pack_weight(n((K, T)) * s, "e4m3")
    return {
        "x_words": x[0],
        "x_scales": x[1],
        "w": (n((E, K, N)) / np.sqrt(K) / s[None] * v[None, None, :]).astype(np.float32),
        "b": (0.3 * n((N, E)) * v[:, None]).astype(np.float32),
        "wp": (n((N, M)) / np.sqrt(N) / v[:, None]).astype(np.float32),
        "gate": np.stack([np.tile(g, (N, 1)), np.tile(1.0 - g, (N, 1))]).astype(np.float32),
        "offs": striped(slot_token),
        "pos1": striped(pos[0]),
        "pos2": striped(pos[1]),
    }


def reference(x_words, x_scales, w, b, wp, gate, offs, pos1, pos2):
    idx = unstriped(offs)
    xq = unpack_weight(x_words, x_scales, "e4m3")[:, idx]
    y = by_expert(mxq(f64(w), 1, "e4m3"), xq)
    y = relu(y + np.repeat(f64(b), C, axis=1))
    c = f64(gate[0]) * y[:, unstriped(pos1)] + f64(gate[1]) * y[:, unstriped(pos2)]
    return mxq(f64(wp), 0, "e4m3").T @ mxq(c, 0, "e4m3")

@@ -1,0 +1,217 @@
+from contextlib import ExitStack
+
+import concourse.mybir as mybir
+from concourse.masks import make_identity
+
+K, T, E, C, N, M = 512, 640, 5, 256, 512, 512
+S = E * C
+FLOPS = 2 * K * N * S + 2 * N * M * T
+BYTES = K * T + 16 * T + 4 * (E * K * N + N * E + N * M + 2 * T + M * T) + 2 * 128 * (S + 2 * T) // 16
+
+F32 = mybir.dt.float32
+BF16 = mybir.dt.bfloat16
+I32 = mybir.dt.int32
+U32 = mybir.dt.uint32
+U16 = mybir.dt.uint16
+U8 = mybir.dt.uint8
+FP8X4 = mybir.dt.float8_e4m3fn_x4
+ACT = mybir.ActivationFunctionType
+ALU = mybir.AluOpType
+
+P = 128
+PACK = 4
+SCALAR_SHARE = (128, 128, 0, 32, 0)
+SLOT_PIECES = ((0, 448), (448, 864), (864, 1280))
+GROUPS = ((0, 256), (256, 384), (384, 512), (512, 576), (576, 640))
+TURNED_TOKENS = 512
+
+
+def tile_moe_nxt_lin_relu_kernel(
+    tc, x_words, x_scales, w, b, wp, gate, offs, pos1, pos2, out
+):
+    nc = tc.nc
+    with ExitStack() as ctx:
+        lists = ctx.enter_context(tc.tile_pool(name="lists", bufs=1))
+        keep = ctx.enter_context(tc.tile_pool(name="keep", bufs=1))
+        psum = ctx.enter_context(tc.psum_pool(name="psum", bufs=1))
+
+        offs_sb = lists.tile([P, S // 16], U16, name="offs_sb")
+        pos_sb = [lists.tile([P, T // 16], U16, name=f"pos_sb{r}") for r in range(2)]
+        xw = keep.tile([P, T], I32, name="xw")
+        xs = keep.tile([P, T], U8, name="xs")
+        bias = keep.tile([P, PACK, E], F32, name="bias")
+        gates = [keep.tile([P, T], F32, name=f"gates{r}") for r in range(2)]
+        ident = keep.tile([P, P], F32, name="ident")
+        w_first = [keep.tile([P, PACK, N // 2], F32, name=f"w_first{h}") for h in range(2)]
+        w_raw = {e: keep.tile([P, PACK, N], F32, name=f"w_raw{e}") for e in range(1, E)}
+        wp_raw = keep.tile([P, PACK, M], F32, name="wp_raw", tag="after_wp", align_bytes=64)
+
+        nc.vector.memset(xs[:].bitcast(I32), 0)
+        make_identity(nc, ident[:])
+
+        def w_rows(e):
+            return w[e].rearrange("(p j) n -> p j n", j=PACK)
+
+        nc.sync.dma_start(offs_sb[:], offs)
+        nc.sync.dma_start(out=xw[:], in_=x_words[0].rearrange("p t r -> p (t r)").bitcast(I32))
+        for r in range(4):
+            nc.sync.dma_start(out=xs[:].bitcast(I32)[r:P:32, :], in_=x_scales[0].bitcast(I32)[r:16:4, :])
+        for h in range(2):
+            nc.sync.dma_start(out=w_first[h][:], in_=w_rows(0)[:, :, h * N // 2 : (h + 1) * N // 2])
+        nc.sync.dma_start(out=w_raw[1][:], in_=w_rows(1))
+        nc.sync.dma_start(out=bias[:], in_=b.rearrange("(p t) e -> p t e", t=PACK))
+        for e in range(2, E):
+            nc.sync.dma_start(out=w_raw[e][:], in_=w_rows(e))
+        nc.sync.dma_start(pos_sb[0][:], pos1)
+        nc.sync.dma_start(pos_sb[1][:], pos2)
+        for r in range(2):
+            nc.sync.dma_start(out=gates[r][:], in_=gate[r, 0:P, :])
+        nc.sync.dma_start(out=wp_raw[:], in_=wp.rearrange("(p j) f -> p j f", j=PACK))
+
+        slot_words = keep.tile([P, S], U32, name="slot_words", align_bytes=64)
+        slot_scales = keep.tile([P, S], U8, name="slot_scales", align_bytes=64)
+        for lo, hi in SLOT_PIECES:
+            entries = offs_sb[:, lo // 16 : hi // 16]
+            nc.vector.tensor_copy(slot_words[:, lo:hi], xw[:].bitcast(U32).indirect(entries))
+            nc.vector.tensor_copy(slot_scales[:, lo:hi], xs[:].indirect(entries))
+
+        def quantize(grouped, name, calls):
+            width = grouped.shape[1] // PACK
+            codes = keep.tile([P, width], U32, name=f"{name}_codes", align_bytes=64)
+            scales = keep.tile([P, width], U8, name=f"{name}_scales", align_bytes=64)
+            step = width // calls
+            for lo in range(0, width, step):
+                nc.vector.quantize_mx(
+                    out=codes[:, lo : lo + step].bitcast(FP8X4),
+                    scales=scales[:, lo : lo + step],
+                    in_=grouped[:, PACK * lo : PACK * (lo + step)],
+                )
+            return codes, scales
+
+        y = [keep.tile([P, S], F32, name=f"y{t}") for t in range(PACK)]
+        for e in range(E):
+            grouped = keep.tile([P, N * PACK], BF16, name=f"w{e}_bf16", align_bytes=64)
+            dst = grouped[:].rearrange("p (t m j) -> p m j t", t=PACK, j=PACK)
+            if e == 0:
+                for h in range(2):
+                    src = w_first[h][:].rearrange("p j (m t) -> p m j t", t=PACK)
+                    nc.scalar.copy(out=dst[:, h * P // 2 : (h + 1) * P // 2], in_=src)
+            else:
+                src = w_raw[e][:].rearrange("p j (m t) -> p m j t", t=PACK)
+                cut = SCALAR_SHARE[e]
+                if cut > 0:
+                    nc.scalar.copy(out=dst[:, 0:cut], in_=src[:, 0:cut])
+                if cut < P:
+                    nc.vector.tensor_copy(out=dst[:, cut:P], in_=src[:, cut:P])
+            last = e == E - 1
+            codes, scales = quantize(grouped, f"w{e}", PACK if last else 1)
+            slots = slice(e * C, (e + 1) * C)
+            share = 1 if last else 2
+            for first in range(0, PACK, share):
+                acc = psum.tile([P, share, C], F32, name="acc", bufs=4)
+                for i in range(share):
+                    cols = slice((first + i) * P, (first + i + 1) * P)
+                    nc.tensor.matmul_mx(
+                        out=acc[:, i, :],
+                        lhsT=codes[:, cols].bitcast(FP8X4),
+                        lhsT_scale=scales[:, cols],
+                        rhs=slot_words[:, slots].bitcast(FP8X4),
+                        rhs_scale=slot_scales[:, slots],
+                        start=True,
+                        stop=True,
+                    )
+                for i in range(share):
+                    t = first + i
+                    nc.scalar.activation(out=y[t][:, slots], in_=acc[:, i, :], func=ACT.Relu, bias=bias[:, t, e : e + 1])
+
+        def pick(room, lo, hi):
+            width = hi - lo
+            for t in range(PACK):
+                for r in range(2):
+                    at = (r * PACK + t) * width
+                    window = y[t][:].indirect(pos_sb[r][:, lo // 16 : hi // 16])
+                    nc.vector.tensor_tensor(room[:, at : at + width], window, gates[r][:, lo:hi], ALU.mult)
+
+        def add_on_tensor(room, width, grouped, name):
+            back = psum.tile([P, 2, width], F32, name="back", bufs=2)
+            for first in range(0, width, P):
+                turned = psum.tile([P, PACK, P], F32, name="turned", bufs=2)
+                for t in range(PACK):
+                    for r in range(2):
+                        at = (r * PACK + t) * width + first
+                        nc.tensor.matmul(
+                            turned[:, t, :], lhsT=room[:, at : at + P], rhs=ident[:], start=(r == 0), stop=(r == 1), is_transpose=True
+                        )
+                c_tok = keep.tile([P, N], BF16, name=f"c_tok{name}_{first}")
+                nc.scalar.copy(
+                    out=c_tok[:].rearrange("q (u p e) -> q u p e", u=2, e=2),
+                    in_=turned[:].rearrange("q (u e) p -> q u p e", e=2),
+                )
+                words = c_tok[:].bitcast(F32)
+                for u in range(2):
+                    nc.tensor.transpose(back[:, u, first : first + P], words[:, u * P : (u + 1) * P], ident[:])
+            nc.scalar.copy(
+                out=grouped[:].bitcast(F32).rearrange("p (q u) -> p q u", u=2), in_=back[:].rearrange("p u q -> p q u")
+            )
+
+        def add_on_vector(room, width, grouped):
+            walk = "p (t c i) -> p c t i"
+            nc.vector.tensor_tensor(
+                grouped[:].rearrange("p (c i t) -> p c t i", i=4, t=PACK),
+                room[:, 0 : PACK * width].rearrange(walk, t=PACK, i=4),
+                room[:, PACK * width : 2 * PACK * width].rearrange(walk, t=PACK, i=4),
+                ALU.add,
+            )
+
+        out_rows = out.rearrange("(f p) t -> p f t", p=P)
+
+        def project(grouped, lo, hi, wp_codes, wp_scales):
+            codes, scales = quantize(grouped, f"c{lo}", 1)
+            width = hi - lo
+            parts = 2 if width > P or hi == T else 1
+            blocks = M // P // parts
+            for part in range(parts):
+                proj = psum.tile([P, blocks, width], F32, name="acc", bufs=4)
+                for i in range(blocks):
+                    cols = slice((part * blocks + i) * P, (part * blocks + i + 1) * P)
+                    nc.tensor.matmul_mx(
+                        out=proj[:, i, :],
+                        lhsT=wp_codes[:, cols].bitcast(FP8X4),
+                        lhsT_scale=wp_scales[:, cols],
+                        rhs=codes[:].bitcast(FP8X4),
+                        rhs_scale=scales[:],
+                        start=True,
+                        stop=True,
+                    )
+                result = keep.tile([P, blocks, width], F32, name=f"result{lo}_{part}")
+                if hi == T and part == 0:
+                    nc.vector.tensor_copy(out=result[:], in_=proj[:])
+                else:
+                    nc.scalar.copy(out=result[:], in_=proj[:])
+                nc.sync.dma_start(out=out_rows[:, part * blocks : (part + 1) * blocks, lo:hi], in_=result[:])
+
+        for g, (lo, hi) in enumerate(GROUPS):
+            width = hi - lo
+            if g == 0:
+                room = keep.tile([P, 2 * PACK * width], F32, name="picked0")
+            elif g == 1:
+                pair = keep.tile([P, 2 * 2 * PACK * width], F32, name="picked12", tag="after_wp", align_bytes=64)
+                room = pair[:, 0 : 2 * PACK * width]
+            elif g == 2:
+                room = pair[:, 2 * PACK * width : 2 * 2 * PACK * width]
+            else:
+                room = keep.tile([P, 2 * PACK * width], F32, name=f"picked{g}", tag=f"after_c{g - 3}", align_bytes=64)
+            pick(room, lo, hi)
+            if g == 0:
+                wp_grouped = keep.tile([P, M * PACK], BF16, name="wp_bf16", align_bytes=64)
+                nc.scalar.copy(
+                    out=wp_grouped[:].rearrange("p (c i j) -> p c j i", i=4, j=PACK),
+                    in_=wp_raw[:].rearrange("p j (c i) -> p c j i", i=4),
+                )
+                wp_codes, wp_scales = quantize(wp_grouped, "wp", 1)
+            grouped = keep.tile([P, width * PACK], BF16, name=f"c{g}_bf16", tag=f"after_c{g}", align_bytes=64)
+            if hi <= TURNED_TOKENS:
+                add_on_tensor(room, width, grouped, g)
+            else:
+                add_on_vector(room, width, grouped)
+            project(grouped, lo, hi, wp_codes, wp_scales)

@@ -1,7 +1,6 @@
 from contextlib import ExitStack
 
 import concourse.mybir as mybir
-from concourse.masks import make_identity
 
 K, T, E, C, N, M = 512, 640, 5, 256, 512, 512
 S = E * C
@@ -22,8 +21,8 @@ P = 128
 PACK = 4
 SCALAR_SHARE = (128, 128, 0, 32, 0)
 SLOT_PIECES = ((0, 448), (448, 864), (864, 1280))
-GROUPS = ((0, 256), (256, 384), (384, 512), (512, 576), (576, 640))
-TURNED_TOKENS = 512
+GROUPS = ((0, 256), (256, 512), (512, 576), (576, 640))
+TURNED_TOKENS = 0
 
 
 def tile_moe_nxt_lin_relu_kernel(
@@ -41,13 +40,11 @@ def tile_moe_nxt_lin_relu_kernel(
         xs = keep.tile([P, T], U8, name="xs")
         bias = keep.tile([P, PACK, E], F32, name="bias")
         gates = [keep.tile([P, T], F32, name=f"gates{r}") for r in range(2)]
-        ident = keep.tile([P, P], F32, name="ident")
         w_first = [keep.tile([P, PACK, N // 2], F32, name=f"w_first{h}") for h in range(2)]
         w_raw = {e: keep.tile([P, PACK, N], F32, name=f"w_raw{e}") for e in range(1, E)}
-        wp_raw = keep.tile([P, PACK, M], F32, name="wp_raw", tag="after_wp", align_bytes=64)
+        wp_raw = keep.tile([P, PACK, M], F32, name="wp_raw")
 
         nc.vector.memset(xs[:].bitcast(I32), 0)
-        make_identity(nc, ident[:])
 
         def w_rows(e):
             return w[e].rearrange("(p j) n -> p j n", j=PACK)
@@ -108,7 +105,7 @@ def tile_moe_nxt_lin_relu_kernel(
             slots = slice(e * C, (e + 1) * C)
             share = 1 if last else 2
             for first in range(0, PACK, share):
-                acc = psum.tile([P, share, C], F32, name="acc", bufs=4)
+                acc = psum.tile([P, share, C], F32, name="acc", bufs=8)
                 for i in range(share):
                     cols = slice((first + i) * P, (first + i + 1) * P)
                     nc.tensor.matmul_mx(
@@ -132,28 +129,6 @@ def tile_moe_nxt_lin_relu_kernel(
                     window = y[t][:].indirect(pos_sb[r][:, lo // 16 : hi // 16])
                     nc.vector.tensor_tensor(room[:, at : at + width], window, gates[r][:, lo:hi], ALU.mult)
 
-        def add_on_tensor(room, width, grouped, name):
-            back = psum.tile([P, 2, width], F32, name="back", bufs=2)
-            for first in range(0, width, P):
-                turned = psum.tile([P, PACK, P], F32, name="turned", bufs=2)
-                for t in range(PACK):
-                    for r in range(2):
-                        at = (r * PACK + t) * width + first
-                        nc.tensor.matmul(
-                            turned[:, t, :], lhsT=room[:, at : at + P], rhs=ident[:], start=(r == 0), stop=(r == 1), is_transpose=True
-                        )
-                c_tok = keep.tile([P, N], BF16, name=f"c_tok{name}_{first}")
-                nc.scalar.copy(
-                    out=c_tok[:].rearrange("q (u p e) -> q u p e", u=2, e=2),
-                    in_=turned[:].rearrange("q (u e) p -> q u p e", e=2),
-                )
-                words = c_tok[:].bitcast(F32)
-                for u in range(2):
-                    nc.tensor.transpose(back[:, u, first : first + P], words[:, u * P : (u + 1) * P], ident[:])
-            nc.scalar.copy(
-                out=grouped[:].bitcast(F32).rearrange("p (q u) -> p q u", u=2), in_=back[:].rearrange("p u q -> p q u")
-            )
-
         def add_on_vector(room, width, grouped):
             walk = "p (t c i) -> p c t i"
             nc.vector.tensor_tensor(
@@ -171,7 +146,7 @@ def tile_moe_nxt_lin_relu_kernel(
             parts = 2 if width > P or hi == T else 1
             blocks = M // P // parts
             for part in range(parts):
-                proj = psum.tile([P, blocks, width], F32, name="acc", bufs=4)
+                proj = psum.tile([P, blocks, width], F32, name="acc", bufs=8)
                 for i in range(blocks):
                     cols = slice((part * blocks + i) * P, (part * blocks + i + 1) * P)
                     nc.tensor.matmul_mx(
@@ -190,17 +165,10 @@ def tile_moe_nxt_lin_relu_kernel(
                     nc.scalar.copy(out=result[:], in_=proj[:])
                 nc.sync.dma_start(out=out_rows[:, part * blocks : (part + 1) * blocks, lo:hi], in_=result[:])
 
+        rooms = [keep.tile([P, 2 * PACK * 256], F32, name=f"room{i}") for i in range(2)]
         for g, (lo, hi) in enumerate(GROUPS):
             width = hi - lo
-            if g == 0:
-                room = keep.tile([P, 2 * PACK * width], F32, name="picked0")
-            elif g == 1:
-                pair = keep.tile([P, 2 * 2 * PACK * width], F32, name="picked12", tag="after_wp", align_bytes=64)
-                room = pair[:, 0 : 2 * PACK * width]
-            elif g == 2:
-                room = pair[:, 2 * PACK * width : 2 * 2 * PACK * width]
-            else:
-                room = keep.tile([P, 2 * PACK * width], F32, name=f"picked{g}", tag=f"after_c{g - 3}", align_bytes=64)
+            room = rooms[g % 2]
             pick(room, lo, hi)
             if g == 0:
                 wp_grouped = keep.tile([P, M * PACK], BF16, name="wp_bf16", align_bytes=64)
@@ -209,9 +177,6 @@ def tile_moe_nxt_lin_relu_kernel(
                     in_=wp_raw[:].rearrange("p j (c i) -> p c j i", i=4),
                 )
                 wp_codes, wp_scales = quantize(wp_grouped, "wp", 1)
-            grouped = keep.tile([P, width * PACK], BF16, name=f"c{g}_bf16", tag=f"after_c{g}", align_bytes=64)
-            if hi <= TURNED_TOKENS:
-                add_on_tensor(room, width, grouped, g)
-            else:
-                add_on_vector(room, width, grouped)
+            grouped = keep.tile([P, width * PACK], BF16, name=f"c{g}_bf16", align_bytes=64)
+            add_on_vector(room, width, grouped)
             project(grouped, lo, hi, wp_codes, wp_scales)

@@ -1,6 +1,7 @@
 from contextlib import ExitStack
 
 import concourse.mybir as mybir
+from concourse.masks import make_identity
 
 K, T, E, C, N, M = 512, 640, 5, 256, 512, 512
 S = E * C
@@ -21,8 +22,8 @@ P = 128
 PACK = 4
 SCALAR_SHARE = (128, 128, 0, 32, 0)
 SLOT_PIECES = ((0, 448), (448, 864), (864, 1280))
-GROUPS = ((0, 256), (256, 512), (512, 576), (576, 640))
-TURNED_TOKENS = 0
+GROUPS = ((0, 384), (384, 512), (512, 640))
+TURNED_TOKENS = 384
 
 
 def tile_moe_nxt_lin_relu_kernel(
@@ -40,11 +41,13 @@ def tile_moe_nxt_lin_relu_kernel(
         xs = keep.tile([P, T], U8, name="xs")
         bias = keep.tile([P, PACK, E], F32, name="bias")
         gates = [keep.tile([P, T], F32, name=f"gates{r}") for r in range(2)]
+        ident = keep.tile([P, P], F32, name="ident")
         w_first = [keep.tile([P, PACK, N // 2], F32, name=f"w_first{h}") for h in range(2)]
         w_raw = {e: keep.tile([P, PACK, N], F32, name=f"w_raw{e}") for e in range(1, E)}
-        wp_raw = keep.tile([P, PACK, M], F32, name="wp_raw")
+        wp_raw = [keep.tile([P, PACK, M // 2], F32, name=f"wp_raw{h}", tag=f"after_wp{h}") for h in range(2)]
 
         nc.vector.memset(xs[:].bitcast(I32), 0)
+        make_identity(nc, ident[:])
 
         def w_rows(e):
             return w[e].rearrange("(p j) n -> p j n", j=PACK)
@@ -63,7 +66,9 @@ def tile_moe_nxt_lin_relu_kernel(
         nc.sync.dma_start(pos_sb[1][:], pos2)
         for r in range(2):
             nc.sync.dma_start(out=gates[r][:], in_=gate[r, 0:P, :])
-        nc.sync.dma_start(out=wp_raw[:], in_=wp.rearrange("(p j) f -> p j f", j=PACK))
+        for h in range(2):
+            rows = wp.rearrange("(p j) f -> p j f", j=PACK)
+            nc.sync.dma_start(out=wp_raw[h][:], in_=rows[:, :, h * M // 2 : (h + 1) * M // 2])
 
         slot_words = keep.tile([P, S], U32, name="slot_words", align_bytes=64)
         slot_scales = keep.tile([P, S], U8, name="slot_scales", align_bytes=64)
@@ -72,9 +77,9 @@ def tile_moe_nxt_lin_relu_kernel(
             nc.vector.tensor_copy(slot_words[:, lo:hi], xw[:].bitcast(U32).indirect(entries))
             nc.vector.tensor_copy(slot_scales[:, lo:hi], xs[:].indirect(entries))
 
-        def quantize(grouped, name, calls):
+        def quantize(grouped, name, calls, tag=""):
             width = grouped.shape[1] // PACK
-            codes = keep.tile([P, width], U32, name=f"{name}_codes", align_bytes=64)
+            codes = keep.tile([P, width], U32, name=f"{name}_codes", tag=tag, align_bytes=64)
             scales = keep.tile([P, width], U8, name=f"{name}_scales", align_bytes=64)
             step = width // calls
             for lo in range(0, width, step):
@@ -101,11 +106,11 @@ def tile_moe_nxt_lin_relu_kernel(
                 if cut < P:
                     nc.vector.tensor_copy(out=dst[:, cut:P], in_=src[:, cut:P])
             last = e == E - 1
-            codes, scales = quantize(grouped, f"w{e}", PACK if last else 1)
+            codes, scales = quantize(grouped, f"w{e}", PACK if last else 1, "after_experts" if last else "")
             slots = slice(e * C, (e + 1) * C)
             share = 1 if last else 2
             for first in range(0, PACK, share):
-                acc = psum.tile([P, share, C], F32, name="acc", bufs=8)
+                acc = psum.tile([P, share, C], F32, name="acc", bufs=3)
                 for i in range(share):
                     cols = slice((first + i) * P, (first + i + 1) * P)
                     nc.tensor.matmul_mx(
@@ -129,13 +134,31 @@ def tile_moe_nxt_lin_relu_kernel(
                     window = y[t][:].indirect(pos_sb[r][:, lo // 16 : hi // 16])
                     nc.vector.tensor_tensor(room[:, at : at + width], window, gates[r][:, lo:hi], ALU.mult)
 
-        def add_on_vector(room, width, grouped):
-            walk = "p (t c i) -> p c t i"
+        def add_on_tensor(room, width, skip, grouped, j):
+            turned = psum.tile([P, PACK, P], F32, name="turned", bufs=3)
+            for t in range(PACK):
+                for r in range(2):
+                    at = (r * PACK + t) * width + skip
+                    nc.tensor.matmul(
+                        turned[:, t, :], lhsT=room[:, at : at + P], rhs=ident[:], start=(r == 0), stop=(r == 1), is_transpose=True
+                    )
+            c_tok = keep.tile([P, N], BF16, name=f"c_tok{j}", tag="after_wp0" if j == 0 else "")
+            nc.scalar.copy(
+                out=c_tok[:].rearrange("q (u p e) -> q u p e", u=2, e=2),
+                in_=turned[:].rearrange("q (u e) p -> q u p e", e=2),
+            )
+            words = c_tok[:].bitcast(F32)
+            back = psum.tile([P, 2, P], F32, name="back", bufs=2)
+            for u in range(2):
+                nc.tensor.transpose(back[:, u, :], words[:, u * P : (u + 1) * P], ident[:])
+            nc.scalar.copy(
+                out=grouped[:].bitcast(F32).rearrange("p (q u) -> p q u", u=2), in_=back[:].rearrange("p u q -> p q u")
+            )
+
+        def add_on_vector(room, grouped):
+            both = room[:].rearrange("p (r t c i) -> p r c t i", r=2, t=PACK, i=4)
             nc.vector.tensor_tensor(
-                grouped[:].rearrange("p (c i t) -> p c t i", i=4, t=PACK),
-                room[:, 0 : PACK * width].rearrange(walk, t=PACK, i=4),
-                room[:, PACK * width : 2 * PACK * width].rearrange(walk, t=PACK, i=4),
-                ALU.add,
+                grouped[:].rearrange("p (c i t) -> p c t i", i=4, t=PACK), both[:, 0], both[:, 1], ALU.add
             )
 
         out_rows = out.rearrange("(f p) t -> p f t", p=P)
@@ -146,7 +169,7 @@ def tile_moe_nxt_lin_relu_kernel(
             parts = 2 if width > P or hi == T else 1
             blocks = M // P // parts
             for part in range(parts):
-                proj = psum.tile([P, blocks, width], F32, name="acc", bufs=8)
+                proj = psum.tile([P, blocks, width], F32, name="acc", bufs=3)
                 for i in range(blocks):
                     cols = slice((part * blocks + i) * P, (part * blocks + i + 1) * P)
                     nc.tensor.matmul_mx(
@@ -163,20 +186,26 @@ def tile_moe_nxt_lin_relu_kernel(
                     nc.vector.tensor_copy(out=result[:], in_=proj[:])
                 else:
                     nc.scalar.copy(out=result[:], in_=proj[:])
-                nc.sync.dma_start(out=out_rows[:, part * blocks : (part + 1) * blocks, lo:hi], in_=result[:])
+                queue = nc.scalar if hi == T and part == 1 else nc.sync
+                queue.dma_start(out=out_rows[:, part * blocks : (part + 1) * blocks, lo:hi], in_=result[:])
 
-        rooms = [keep.tile([P, 2 * PACK * 256], F32, name=f"room{i}") for i in range(2)]
-        for g, (lo, hi) in enumerate(GROUPS):
-            width = hi - lo
-            room = rooms[g % 2]
+        room = keep.tile([P, 2 * PACK * GROUPS[0][1]], F32, name="first_room")
+        for lo, hi in GROUPS:
+            if lo == GROUPS[1][0]:
+                room = keep.tile([P, 2 * PACK * P], F32, name="room", tag="after_wp1")
             pick(room, lo, hi)
-            if g == 0:
-                wp_grouped = keep.tile([P, M * PACK], BF16, name="wp_bf16", align_bytes=64)
-                nc.scalar.copy(
-                    out=wp_grouped[:].rearrange("p (c i j) -> p c j i", i=4, j=PACK),
-                    in_=wp_raw[:].rearrange("p j (c i) -> p c j i", i=4),
-                )
+            if lo == 0:
+                wp_grouped = keep.tile([P, M * PACK], BF16, name="wp_bf16", tag="after_experts", align_bytes=64)
+                for h in range(2):
+                    nc.scalar.copy(
+                        out=wp_grouped[:, h * 2 * M : (h + 1) * 2 * M].rearrange("p (c i j) -> p c j i", i=4, j=PACK),
+                        in_=wp_raw[h][:].rearrange("p j (c i) -> p c j i", i=4),
+                    )
                 wp_codes, wp_scales = quantize(wp_grouped, "wp", 1)
-            grouped = keep.tile([P, width * PACK], BF16, name=f"c{g}_bf16", align_bytes=64)
-            add_on_vector(room, width, grouped)
-            project(grouped, lo, hi, wp_codes, wp_scales)
+            for first in range(lo, hi, P):
+                grouped = keep.tile([P, P * PACK], BF16, name=f"c{first}_bf16", align_bytes=64)
+                if first < TURNED_TOKENS:
+                    add_on_tensor(room, hi - lo, first - lo, grouped, first // P)
+                else:
+                    add_on_vector(room, grouped)
+                project(grouped, first, first + P, wp_codes, wp_scales)

@@ -20,10 +20,13 @@ ALU = mybir.AluOpType
 
 P = 128
 PACK = 4
-SCALAR_SHARE = (128, 128, 0, 32, 0)
+LINE = 4
+LIST_ROWS = 16
+SCALAR_EXPERTS = 2
 SLOT_PIECES = ((0, 448), (448, 864), (864, 1280))
-GROUPS = ((0, 384), (384, 512), (512, 640))
-TURNED_TOKENS = 384
+TENSOR_TOKENS = 3 * P
+GROUPS = ((0, TENSOR_TOKENS), (TENSOR_TOKENS, TENSOR_TOKENS + P), (TENSOR_TOKENS + P, T))
+SUM_BANKS, TURN_BANKS, BACK_BANKS = 3, 3, 2
 
 
 def tile_moe_nxt_lin_relu_kernel(
@@ -35,54 +38,53 @@ def tile_moe_nxt_lin_relu_kernel(
         keep = ctx.enter_context(tc.tile_pool(name="keep", bufs=1))
         psum = ctx.enter_context(tc.psum_pool(name="psum", bufs=1))
 
-        offs_sb = lists.tile([P, S // 16], U16, name="offs_sb")
-        pos_sb = [lists.tile([P, T // 16], U16, name=f"pos_sb{r}") for r in range(2)]
-        xw = keep.tile([P, T], I32, name="xw")
-        xs = keep.tile([P, T], U8, name="xs")
-        bias = keep.tile([P, PACK, E], F32, name="bias")
+        offs_sb = lists.tile([P, S // LIST_ROWS], U16, name="offs_sb")
+        pos_sb = [lists.tile([P, T // LIST_ROWS], U16, name=f"pos_sb{r}") for r in range(2)]
+        token_words = keep.tile([P, T], I32, name="token_words")
+        token_scales = keep.tile([P, T], U8, name="token_scales")
+        bias = keep.tile([P, PACK, E], F32, name="bias", tag="after_relu", align_bytes=64)
         gates = [keep.tile([P, T], F32, name=f"gates{r}") for r in range(2)]
         ident = keep.tile([P, P], F32, name="ident")
         w_first = [keep.tile([P, PACK, N // 2], F32, name=f"w_first{h}") for h in range(2)]
         w_raw = {e: keep.tile([P, PACK, N], F32, name=f"w_raw{e}") for e in range(1, E)}
         wp_raw = [keep.tile([P, PACK, M // 2], F32, name=f"wp_raw{h}", tag=f"after_wp{h}") for h in range(2)]
 
-        nc.vector.memset(xs[:].bitcast(I32), 0)
+        nc.gpsimd.memset(token_scales[:].bitcast(I32), 0)
         make_identity(nc, ident[:])
 
-        def w_rows(e):
-            return w[e].rearrange("(p j) n -> p j n", j=PACK)
+        def by_words(matrix):
+            return matrix.rearrange("(p j) x -> p j x", j=PACK)
 
         nc.sync.dma_start(offs_sb[:], offs)
-        nc.sync.dma_start(out=xw[:], in_=x_words[0].rearrange("p t r -> p (t r)").bitcast(I32))
+        nc.sync.dma_start(out=token_words[:], in_=x_words[0].rearrange("p t r -> p (t r)").bitcast(I32))
         for r in range(4):
-            nc.sync.dma_start(out=xs[:].bitcast(I32)[r:P:32, :], in_=x_scales[0].bitcast(I32)[r:16:4, :])
+            nc.sync.dma_start(out=token_scales[:].bitcast(I32)[r:P:32, :], in_=x_scales[0].bitcast(I32)[r:16:4, :])
         for h in range(2):
-            nc.sync.dma_start(out=w_first[h][:], in_=w_rows(0)[:, :, h * N // 2 : (h + 1) * N // 2])
-        nc.sync.dma_start(out=w_raw[1][:], in_=w_rows(1))
+            nc.sync.dma_start(out=w_first[h][:], in_=by_words(w[0])[:, :, h * N // 2 : (h + 1) * N // 2])
+        nc.sync.dma_start(out=w_raw[1][:], in_=by_words(w[1]))
         nc.sync.dma_start(out=bias[:], in_=b.rearrange("(p t) e -> p t e", t=PACK))
         for e in range(2, E):
-            nc.sync.dma_start(out=w_raw[e][:], in_=w_rows(e))
+            nc.sync.dma_start(out=w_raw[e][:], in_=by_words(w[e]))
         nc.sync.dma_start(pos_sb[0][:], pos1)
         nc.sync.dma_start(pos_sb[1][:], pos2)
         for r in range(2):
             nc.sync.dma_start(out=gates[r][:], in_=gate[r, 0:P, :])
         for h in range(2):
-            rows = wp.rearrange("(p j) f -> p j f", j=PACK)
-            nc.sync.dma_start(out=wp_raw[h][:], in_=rows[:, :, h * M // 2 : (h + 1) * M // 2])
+            nc.sync.dma_start(out=wp_raw[h][:], in_=by_words(wp)[:, :, h * M // 2 : (h + 1) * M // 2])
 
         slot_words = keep.tile([P, S], U32, name="slot_words", align_bytes=64)
         slot_scales = keep.tile([P, S], U8, name="slot_scales", align_bytes=64)
         for lo, hi in SLOT_PIECES:
-            entries = offs_sb[:, lo // 16 : hi // 16]
-            nc.vector.tensor_copy(slot_words[:, lo:hi], xw[:].bitcast(U32).indirect(entries))
-            nc.vector.tensor_copy(slot_scales[:, lo:hi], xs[:].indirect(entries))
+            entries = offs_sb[:, lo // LIST_ROWS : hi // LIST_ROWS]
+            nc.vector.tensor_copy(slot_words[:, lo:hi], token_words[:].bitcast(U32).indirect(entries))
+            nc.vector.tensor_copy(slot_scales[:, lo:hi], token_scales[:].indirect(entries))
 
-        def quantize(grouped, name, calls, tag=""):
-            width = grouped.shape[1] // PACK
-            codes = keep.tile([P, width], U32, name=f"{name}_codes", tag=tag, align_bytes=64)
-            scales = keep.tile([P, width], U8, name=f"{name}_scales", align_bytes=64)
-            step = width // calls
-            for lo in range(0, width, step):
+        def quantize(grouped, name, calls):
+            columns = grouped.shape[1] // PACK
+            codes = keep.tile([P, columns], U32, name=f"{name}_codes", align_bytes=64)
+            scales = keep.tile([P, columns], U8, name=f"{name}_scales", align_bytes=64)
+            step = columns // calls
+            for lo in range(0, columns, step):
                 nc.vector.quantize_mx(
                     out=codes[:, lo : lo + step].bitcast(FP8X4),
                     scales=scales[:, lo : lo + step],
@@ -90,122 +92,122 @@ def tile_moe_nxt_lin_relu_kernel(
                 )
             return codes, scales
 
+        def multiply(sums, block, codes, scales, moving_words, moving_scales):
+            cols = slice(block * P, (block + 1) * P)
+            nc.tensor.matmul_mx(
+                out=sums,
+                lhsT=codes[:, cols].bitcast(FP8X4),
+                lhsT_scale=scales[:, cols],
+                rhs=moving_words.bitcast(FP8X4),
+                rhs_scale=moving_scales,
+                start=True,
+                stop=True,
+            )
+
         y = [keep.tile([P, S], F32, name=f"y{t}") for t in range(PACK)]
         for e in range(E):
-            grouped = keep.tile([P, N * PACK], BF16, name=f"w{e}_bf16", align_bytes=64)
-            dst = grouped[:].rearrange("p (t m j) -> p m j t", t=PACK, j=PACK)
+            w_grouped = keep.tile([P, N * PACK], BF16, name=f"w{e}_bf16", align_bytes=64)
+            dst = w_grouped[:].rearrange("p (t m j) -> p m j t", t=PACK, j=PACK)
             if e == 0:
                 for h in range(2):
                     src = w_first[h][:].rearrange("p j (m t) -> p m j t", t=PACK)
                     nc.scalar.copy(out=dst[:, h * P // 2 : (h + 1) * P // 2], in_=src)
+            elif e < SCALAR_EXPERTS:
+                nc.scalar.copy(out=dst, in_=w_raw[e][:].rearrange("p j (m t) -> p m j t", t=PACK))
             else:
-                src = w_raw[e][:].rearrange("p j (m t) -> p m j t", t=PACK)
-                cut = SCALAR_SHARE[e]
-                if cut > 0:
-                    nc.scalar.copy(out=dst[:, 0:cut], in_=src[:, 0:cut])
-                if cut < P:
-                    nc.vector.tensor_copy(out=dst[:, cut:P], in_=src[:, cut:P])
+                nc.vector.tensor_copy(out=dst, in_=w_raw[e][:].rearrange("p j (m t) -> p m j t", t=PACK))
             last = e == E - 1
-            codes, scales = quantize(grouped, f"w{e}", PACK if last else 1, "after_experts" if last else "")
+            w_codes, w_scales = quantize(w_grouped, f"w{e}", PACK if last else 1)
             slots = slice(e * C, (e + 1) * C)
-            share = 1 if last else 2
-            for first in range(0, PACK, share):
-                acc = psum.tile([P, share, C], F32, name="acc", bufs=3)
-                for i in range(share):
-                    cols = slice((first + i) * P, (first + i + 1) * P)
-                    nc.tensor.matmul_mx(
-                        out=acc[:, i, :],
-                        lhsT=codes[:, cols].bitcast(FP8X4),
-                        lhsT_scale=scales[:, cols],
-                        rhs=slot_words[:, slots].bitcast(FP8X4),
-                        rhs_scale=slot_scales[:, slots],
-                        start=True,
-                        stop=True,
-                    )
-                for i in range(share):
+            planes_a_bank = 1 if last else 2
+            for first in range(0, PACK, planes_a_bank):
+                sums = psum.tile([P, planes_a_bank, C], F32, name="sums", bufs=SUM_BANKS)
+                for i in range(planes_a_bank):
+                    multiply(sums[:, i, :], first + i, w_codes, w_scales, slot_words[:, slots], slot_scales[:, slots])
+                for i in range(planes_a_bank):
                     t = first + i
-                    nc.scalar.activation(out=y[t][:, slots], in_=acc[:, i, :], func=ACT.Relu, bias=bias[:, t, e : e + 1])
+                    nc.scalar.activation(out=y[t][:, slots], in_=sums[:, i, :], func=ACT.Relu, bias=bias[:, t, e : e + 1])
 
-        def pick(room, lo, hi):
+        def pick(picked, lo, hi):
             width = hi - lo
             for t in range(PACK):
                 for r in range(2):
                     at = (r * PACK + t) * width
-                    window = y[t][:].indirect(pos_sb[r][:, lo // 16 : hi // 16])
-                    nc.vector.tensor_tensor(room[:, at : at + width], window, gates[r][:, lo:hi], ALU.mult)
+                    window = y[t][:].indirect(pos_sb[r][:, lo // LIST_ROWS : hi // LIST_ROWS])
+                    nc.vector.tensor_tensor(picked[:, at : at + width], window, gates[r][:, lo:hi], ALU.mult)
 
-        def add_on_tensor(room, width, skip, grouped, j):
-            turned = psum.tile([P, PACK, P], F32, name="turned", bufs=3)
+        def add_on_tensor(picked, first, c_grouped):
+            turned = psum.tile([P, PACK, P], F32, name="turned", bufs=TURN_BANKS)
             for t in range(PACK):
                 for r in range(2):
-                    at = (r * PACK + t) * width + skip
+                    at = (r * PACK + t) * TENSOR_TOKENS + first
                     nc.tensor.matmul(
-                        turned[:, t, :], lhsT=room[:, at : at + P], rhs=ident[:], start=(r == 0), stop=(r == 1), is_transpose=True
+                        turned[:, t, :],
+                        lhsT=picked[:, at : at + P],
+                        rhs=ident[:],
+                        start=(r == 0),
+                        stop=(r == 1),
+                        is_transpose=True,
                     )
-            c_tok = keep.tile([P, N], BF16, name=f"c_tok{j}", tag="after_wp0" if j == 0 else "")
+            c_tokens = keep.tile([P, N], BF16, name=f"c_tokens{first}", tag="after_wp0" if first == 0 else "")
             nc.scalar.copy(
-                out=c_tok[:].rearrange("q (u p e) -> q u p e", u=2, e=2),
+                out=c_tokens[:].rearrange("q (u p e) -> q u p e", u=2, e=2),
                 in_=turned[:].rearrange("q (u e) p -> q u p e", e=2),
             )
-            words = c_tok[:].bitcast(F32)
-            back = psum.tile([P, 2, P], F32, name="back", bufs=2)
+            pairs = c_tokens[:].bitcast(F32)
+            back = psum.tile([P, 2, P], F32, name="back", bufs=BACK_BANKS)
             for u in range(2):
-                nc.tensor.transpose(back[:, u, :], words[:, u * P : (u + 1) * P], ident[:])
+                nc.tensor.transpose(back[:, u, :], pairs[:, u * P : (u + 1) * P], ident[:])
             nc.scalar.copy(
-                out=grouped[:].bitcast(F32).rearrange("p (q u) -> p q u", u=2), in_=back[:].rearrange("p u q -> p q u")
+                out=c_grouped[:].bitcast(F32).rearrange("p (q u) -> p q u", u=2), in_=back[:].rearrange("p u q -> p q u")
             )
 
-        def add_on_vector(room, grouped):
-            both = room[:].rearrange("p (r t c i) -> p r c t i", r=2, t=PACK, i=4)
+        def add_on_vector(picked, c_grouped):
+            both = picked[:].rearrange("p (r t x i) -> p r x t i", r=2, t=PACK, i=LINE)
             nc.vector.tensor_tensor(
-                grouped[:].rearrange("p (c i t) -> p c t i", i=4, t=PACK), both[:, 0], both[:, 1], ALU.add
+                c_grouped[:].rearrange("p (x i t) -> p x t i", i=LINE, t=PACK), both[:, 0], both[:, 1], ALU.add
             )
 
-        out_rows = out.rearrange("(f p) t -> p f t", p=P)
+        out_blocks = out.rearrange("(f p) t -> p f t", p=P)
 
-        def project(grouped, lo, hi, wp_codes, wp_scales):
-            codes, scales = quantize(grouped, f"c{lo}", 1)
-            width = hi - lo
-            parts = 2 if width > P or hi == T else 1
+        def project(c_grouped, first, wp_codes, wp_scales):
+            c_codes, c_scales = quantize(c_grouped, f"c{first}", 1)
+            parts = 2 if first + P == T else 1
             blocks = M // P // parts
             for part in range(parts):
-                proj = psum.tile([P, blocks, width], F32, name="acc", bufs=3)
+                sums = psum.tile([P, blocks, P], F32, name="sums", bufs=SUM_BANKS)
                 for i in range(blocks):
-                    cols = slice((part * blocks + i) * P, (part * blocks + i + 1) * P)
-                    nc.tensor.matmul_mx(
-                        out=proj[:, i, :],
-                        lhsT=wp_codes[:, cols].bitcast(FP8X4),
-                        lhsT_scale=wp_scales[:, cols],
-                        rhs=codes[:].bitcast(FP8X4),
-                        rhs_scale=scales[:],
-                        start=True,
-                        stop=True,
-                    )
-                result = keep.tile([P, blocks, width], F32, name=f"result{lo}_{part}")
-                if hi == T and part == 0:
-                    nc.vector.tensor_copy(out=result[:], in_=proj[:])
+                    multiply(sums[:, i, :], part * blocks + i, wp_codes, wp_scales, c_codes[:], c_scales[:])
+                result = keep.tile([P, blocks, P], F32, name=f"result{first}_{part}")
+                if part < parts - 1:
+                    nc.vector.tensor_copy(out=result[:], in_=sums[:])
                 else:
-                    nc.scalar.copy(out=result[:], in_=proj[:])
-                queue = nc.scalar if hi == T and part == 1 else nc.sync
-                queue.dma_start(out=out_rows[:, part * blocks : (part + 1) * blocks, lo:hi], in_=result[:])
+                    nc.scalar.copy(out=result[:], in_=sums[:])
+                queue = nc.scalar if part == 1 else nc.sync
+                queue.dma_start(
+                    out=out_blocks[:, part * blocks : (part + 1) * blocks, first : first + P], in_=result[:]
+                )
 
-        room = keep.tile([P, 2 * PACK * GROUPS[0][1]], F32, name="first_room")
-        for lo, hi in GROUPS:
-            if lo == GROUPS[1][0]:
-                room = keep.tile([P, 2 * PACK * P], F32, name="room", tag="after_wp1")
-            pick(room, lo, hi)
-            if lo == 0:
-                wp_grouped = keep.tile([P, M * PACK], BF16, name="wp_bf16", tag="after_experts", align_bytes=64)
-                for h in range(2):
-                    nc.scalar.copy(
-                        out=wp_grouped[:, h * 2 * M : (h + 1) * 2 * M].rearrange("p (c i j) -> p c j i", i=4, j=PACK),
-                        in_=wp_raw[h][:].rearrange("p j (c i) -> p c j i", i=4),
-                    )
-                wp_codes, wp_scales = quantize(wp_grouped, "wp", 1)
-            for first in range(lo, hi, P):
-                grouped = keep.tile([P, P * PACK], BF16, name=f"c{first}_bf16", align_bytes=64)
-                if first < TURNED_TOKENS:
-                    add_on_tensor(room, hi - lo, first - lo, grouped, first // P)
-                else:
-                    add_on_vector(room, grouped)
-                project(grouped, first, first + P, wp_codes, wp_scales)
+        picked_first = keep.tile([P, 2 * PACK * TENSOR_TOKENS], F32, name="picked_first")
+        pick(picked_first, *GROUPS[0])
+
+        wp_grouped = keep.tile([P, M * PACK], BF16, name="wp_bf16", tag="after_relu", align_bytes=64)
+        for h in range(2):
+            half = wp_grouped[:, h * PACK * M // 2 : (h + 1) * PACK * M // 2]
+            nc.scalar.copy(
+                out=half.rearrange("p (x i j) -> p x j i", i=LINE, j=PACK),
+                in_=wp_raw[h][:].rearrange("p j (x i) -> p x j i", i=LINE),
+            )
+        wp_codes, wp_scales = quantize(wp_grouped, "wp", 1)
+
+        for first in range(0, TENSOR_TOKENS, P):
+            c_grouped = keep.tile([P, P * PACK], BF16, name=f"c{first}_bf16", align_bytes=64)
+            add_on_tensor(picked_first, first, c_grouped)
+            project(c_grouped, first, wp_codes, wp_scales)
+
+        picked_later = keep.tile([P, 2 * PACK * P], F32, name="picked_later", tag="after_wp1")
+        for lo, hi in GROUPS[1:]:
+            pick(picked_later, lo, hi)
+            c_grouped = keep.tile([P, P * PACK], BF16, name=f"c{lo}_bf16", align_bytes=64)
+            add_on_vector(picked_later, c_grouped)
+            project(c_grouped, lo, wp_codes, wp_scales)

from contextlib import ExitStack

import concourse.mybir as mybir
from concourse.masks import make_identity

K, T, E, C, N, M = 512, 640, 5, 256, 512, 512
S = E * C
FLOPS = 2 * K * N * S + 2 * N * M * T
BYTES = K * T + 16 * T + 4 * (E * K * N + N * E + N * M + 2 * T + M * T) + 2 * 128 * (S + 2 * T) // 16

F32 = mybir.dt.float32
BF16 = mybir.dt.bfloat16
I32 = mybir.dt.int32
U32 = mybir.dt.uint32
U16 = mybir.dt.uint16
U8 = mybir.dt.uint8
FP8X4 = mybir.dt.float8_e4m3fn_x4
ACT = mybir.ActivationFunctionType
ALU = mybir.AluOpType

P = 128
PACK = 4
LINE = 4
LIST_ROWS = 16
SCALAR_EXPERTS = 2
SLOT_PIECES = ((0, 448), (448, 864), (864, 1280))
TENSOR_TOKENS = 3 * P
GROUPS = ((0, TENSOR_TOKENS), (TENSOR_TOKENS, TENSOR_TOKENS + P), (TENSOR_TOKENS + P, T))
SUM_BANKS, TURN_BANKS, BACK_BANKS = 3, 3, 2


def tile_moe_nxt_lin_relu_kernel(
    tc, x_words, x_scales, w, b, wp, gate, offs, pos1, pos2, out
):
    nc = tc.nc
    with ExitStack() as ctx:
        lists = ctx.enter_context(tc.tile_pool(name="lists", bufs=1))
        keep = ctx.enter_context(tc.tile_pool(name="keep", bufs=1))
        psum = ctx.enter_context(tc.psum_pool(name="psum", bufs=1))

        offs_sb = lists.tile([P, S // LIST_ROWS], U16, name="offs_sb")
        pos_sb = [lists.tile([P, T // LIST_ROWS], U16, name=f"pos_sb{r}") for r in range(2)]
        token_words = keep.tile([P, T], I32, name="token_words")
        token_scales = keep.tile([P, T], U8, name="token_scales")
        bias = keep.tile([P, PACK, E], F32, name="bias", tag="after_relu", align_bytes=64)
        gates = [keep.tile([P, T], F32, name=f"gates{r}") for r in range(2)]
        ident = keep.tile([P, P], F32, name="ident")
        w_first = [keep.tile([P, PACK, N // 2], F32, name=f"w_first{h}") for h in range(2)]
        w_raw = {e: keep.tile([P, PACK, N], F32, name=f"w_raw{e}") for e in range(1, E)}
        wp_raw = [keep.tile([P, PACK, M // 2], F32, name=f"wp_raw{h}", tag=f"after_wp{h}") for h in range(2)]

        nc.gpsimd.memset(token_scales[:].bitcast(I32), 0)
        make_identity(nc, ident[:])

        def by_words(matrix):
            return matrix.rearrange("(p j) x -> p j x", j=PACK)

        nc.sync.dma_start(offs_sb[:], offs)
        nc.sync.dma_start(out=token_words[:], in_=x_words[0].rearrange("p t r -> p (t r)").bitcast(I32))
        for r in range(4):
            nc.sync.dma_start(out=token_scales[:].bitcast(I32)[r:P:32, :], in_=x_scales[0].bitcast(I32)[r:16:4, :])
        for h in range(2):
            nc.sync.dma_start(out=w_first[h][:], in_=by_words(w[0])[:, :, h * N // 2 : (h + 1) * N // 2])
        nc.sync.dma_start(out=w_raw[1][:], in_=by_words(w[1]))
        nc.sync.dma_start(out=bias[:], in_=b.rearrange("(p t) e -> p t e", t=PACK))
        for e in range(2, E):
            nc.sync.dma_start(out=w_raw[e][:], in_=by_words(w[e]))
        nc.sync.dma_start(pos_sb[0][:], pos1)
        nc.sync.dma_start(pos_sb[1][:], pos2)
        for r in range(2):
            nc.sync.dma_start(out=gates[r][:], in_=gate[r, 0:P, :])
        for h in range(2):
            nc.sync.dma_start(out=wp_raw[h][:], in_=by_words(wp)[:, :, h * M // 2 : (h + 1) * M // 2])

        slot_words = keep.tile([P, S], U32, name="slot_words", align_bytes=64)
        slot_scales = keep.tile([P, S], U8, name="slot_scales", align_bytes=64)
        for lo, hi in SLOT_PIECES:
            entries = offs_sb[:, lo // LIST_ROWS : hi // LIST_ROWS]
            nc.vector.tensor_copy(slot_words[:, lo:hi], token_words[:].bitcast(U32).indirect(entries))
            nc.vector.tensor_copy(slot_scales[:, lo:hi], token_scales[:].indirect(entries))

        def quantize(grouped, name, calls):
            columns = grouped.shape[1] // PACK
            codes = keep.tile([P, columns], U32, name=f"{name}_codes", align_bytes=64)
            scales = keep.tile([P, columns], U8, name=f"{name}_scales", align_bytes=64)
            step = columns // calls
            for lo in range(0, columns, step):
                nc.vector.quantize_mx(
                    out=codes[:, lo : lo + step].bitcast(FP8X4),
                    scales=scales[:, lo : lo + step],
                    in_=grouped[:, PACK * lo : PACK * (lo + step)],
                )
            return codes, scales

        def multiply(sums, block, codes, scales, moving_words, moving_scales):
            cols = slice(block * P, (block + 1) * P)
            nc.tensor.matmul_mx(
                out=sums,
                lhsT=codes[:, cols].bitcast(FP8X4),
                lhsT_scale=scales[:, cols],
                rhs=moving_words.bitcast(FP8X4),
                rhs_scale=moving_scales,
                start=True,
                stop=True,
            )

        y = [keep.tile([P, S], F32, name=f"y{t}") for t in range(PACK)]
        for e in range(E):
            w_grouped = keep.tile([P, N * PACK], BF16, name=f"w{e}_bf16", align_bytes=64)
            dst = w_grouped[:].rearrange("p (t m j) -> p m j t", t=PACK, j=PACK)
            if e == 0:
                for h in range(2):
                    src = w_first[h][:].rearrange("p j (m t) -> p m j t", t=PACK)
                    nc.scalar.copy(out=dst[:, h * P // 2 : (h + 1) * P // 2], in_=src)
            elif e < SCALAR_EXPERTS:
                nc.scalar.copy(out=dst, in_=w_raw[e][:].rearrange("p j (m t) -> p m j t", t=PACK))
            else:
                nc.vector.tensor_copy(out=dst, in_=w_raw[e][:].rearrange("p j (m t) -> p m j t", t=PACK))
            last = e == E - 1
            w_codes, w_scales = quantize(w_grouped, f"w{e}", PACK if last else 1)
            slots = slice(e * C, (e + 1) * C)
            planes_a_bank = 1 if last else 2
            for first in range(0, PACK, planes_a_bank):
                sums = psum.tile([P, planes_a_bank, C], F32, name="sums", bufs=SUM_BANKS)
                for i in range(planes_a_bank):
                    multiply(sums[:, i, :], first + i, w_codes, w_scales, slot_words[:, slots], slot_scales[:, slots])
                for i in range(planes_a_bank):
                    t = first + i
                    nc.scalar.activation(out=y[t][:, slots], in_=sums[:, i, :], func=ACT.Relu, bias=bias[:, t, e : e + 1])

        def pick(picked, lo, hi):
            width = hi - lo
            for t in range(PACK):
                for r in range(2):
                    at = (r * PACK + t) * width
                    window = y[t][:].indirect(pos_sb[r][:, lo // LIST_ROWS : hi // LIST_ROWS])
                    nc.vector.tensor_tensor(picked[:, at : at + width], window, gates[r][:, lo:hi], ALU.mult)

        def add_on_tensor(picked, first, c_grouped):
            turned = psum.tile([P, PACK, P], F32, name="turned", bufs=TURN_BANKS)
            for t in range(PACK):
                for r in range(2):
                    at = (r * PACK + t) * TENSOR_TOKENS + first
                    nc.tensor.matmul(
                        turned[:, t, :],
                        lhsT=picked[:, at : at + P],
                        rhs=ident[:],
                        start=(r == 0),
                        stop=(r == 1),
                        is_transpose=True,
                    )
            c_tokens = keep.tile([P, N], BF16, name=f"c_tokens{first}", tag="after_wp0" if first == 0 else "")
            nc.scalar.copy(
                out=c_tokens[:].rearrange("q (u p e) -> q u p e", u=2, e=2),
                in_=turned[:].rearrange("q (u e) p -> q u p e", e=2),
            )
            pairs = c_tokens[:].bitcast(F32)
            back = psum.tile([P, 2, P], F32, name="back", bufs=BACK_BANKS)
            for u in range(2):
                nc.tensor.transpose(back[:, u, :], pairs[:, u * P : (u + 1) * P], ident[:])
            nc.scalar.copy(
                out=c_grouped[:].bitcast(F32).rearrange("p (q u) -> p q u", u=2), in_=back[:].rearrange("p u q -> p q u")
            )

        def add_on_vector(picked, c_grouped):
            both = picked[:].rearrange("p (r t x i) -> p r x t i", r=2, t=PACK, i=LINE)
            nc.vector.tensor_tensor(
                c_grouped[:].rearrange("p (x i t) -> p x t i", i=LINE, t=PACK), both[:, 0], both[:, 1], ALU.add
            )

        out_blocks = out.rearrange("(f p) t -> p f t", p=P)

        def project(c_grouped, first, wp_codes, wp_scales):
            c_codes, c_scales = quantize(c_grouped, f"c{first}", 1)
            parts = 2 if first + P == T else 1
            blocks = M // P // parts
            for part in range(parts):
                sums = psum.tile([P, blocks, P], F32, name="sums", bufs=SUM_BANKS)
                for i in range(blocks):
                    multiply(sums[:, i, :], part * blocks + i, wp_codes, wp_scales, c_codes[:], c_scales[:])
                result = keep.tile([P, blocks, P], F32, name=f"result{first}_{part}")
                if part < parts - 1:
                    nc.vector.tensor_copy(out=result[:], in_=sums[:])
                else:
                    nc.scalar.copy(out=result[:], in_=sums[:])
                queue = nc.scalar if part == 1 else nc.sync
                queue.dma_start(
                    out=out_blocks[:, part * blocks : (part + 1) * blocks, first : first + P], in_=result[:]
                )

        picked_first = keep.tile([P, 2 * PACK * TENSOR_TOKENS], F32, name="picked_first")
        pick(picked_first, *GROUPS[0])

        wp_grouped = keep.tile([P, M * PACK], BF16, name="wp_bf16", tag="after_relu", align_bytes=64)
        for h in range(2):
            half = wp_grouped[:, h * PACK * M // 2 : (h + 1) * PACK * M // 2]
            nc.scalar.copy(
                out=half.rearrange("p (x i j) -> p x j i", i=LINE, j=PACK),
                in_=wp_raw[h][:].rearrange("p j (x i) -> p x j i", i=LINE),
            )
        wp_codes, wp_scales = quantize(wp_grouped, "wp", 1)

        for first in range(0, TENSOR_TOKENS, P):
            c_grouped = keep.tile([P, P * PACK], BF16, name=f"c{first}_bf16", align_bytes=64)
            add_on_tensor(picked_first, first, c_grouped)
            project(c_grouped, first, wp_codes, wp_scales)

        picked_later = keep.tile([P, 2 * PACK * P], F32, name="picked_later", tag="after_wp1")
        for lo, hi in GROUPS[1:]:
            pick(picked_later, lo, hi)
            c_grouped = keep.tile([P, P * PACK], BF16, name=f"c{lo}_bf16", align_bytes=64)
            add_on_vector(picked_later, c_grouped)
            project(c_grouped, lo, wp_codes, wp_scales)
